import numpy as np
import ml_dtypes


def mxq(x, axis, fmt="e4m3"):
    dtype, down = {"e4m3": (ml_dtypes.float8_e4m3fn, 7), "e5m2": (ml_dtypes.float8_e5m2, 14)}[fmt]
    v = np.moveaxis(np.asarray(x, np.float32).astype(ml_dtypes.bfloat16).astype(np.float64), axis, -1)
    blocks = v.reshape(v.shape[:-1] + (-1, 32))
    amax = np.abs(blocks).max(-1, keepdims=True)
    byte = np.maximum(np.where(amax > 0, np.frexp(amax)[1] - 1 + 127, 0) - down, 1)
    scale = np.exp2(byte - 127.0)
    codes = (blocks / scale).astype(np.float32).astype(dtype).astype(np.float64)
    return np.moveaxis((codes * scale).reshape(v.shape), -1, axis)


WIDE = False


def mx_kscale(k):
    if not WIDE:
        return np.ones(k)
    levels = np.array([10, -10, 5, -5, 0])
    if k % 512:
        return np.exp2(np.random.permutation(np.resize(levels, k // 32))).repeat(32)
    a = np.empty((k // 512, 16))
    for p in range(k // 512):
        a[p, :8] = np.random.permutation(np.resize(levels, 8))
        for g in range(8):
            far = levels[np.abs(levels - a[p, g]) >= 10]
            a[p, g + 8] = far[np.random.randint(len(far))]
    return np.exp2(a.ravel()).repeat(32)


def f64(x):
    return np.asarray(x).astype(np.float64)


def striped(idx):
    return np.tile(idx.reshape(-1, 16).T, (8, 1)).astype(np.uint16)


def unstriped(offs):
    return offs[:16].T.reshape(-1).astype(np.int64)


E2M1 = np.array([0.0, 0.5, 1.0, 1.5, 2.0, 3.0, 4.0, 6.0, -0.0, -0.5, -1.0, -1.5, -2.0, -3.0, -4.0, -6.0])


def pack_weight(w, fmt):
    k, n = w.shape
    w = f64(np.asarray(w, np.float32).astype(ml_dtypes.bfloat16)).reshape(k // 32, 32, n)
    amax = np.abs(w).max(1)
    if fmt == "e4m3":
        byte = np.frexp(amax)[1] - 1 + 127 - 7
    else:
        mant, ex = np.frexp(amax / 6.0)
        byte = np.where(mant > 0.5, ex, ex - 1) + 127
    byte = np.clip(np.where(amax > 0, byte, 1), 1, 254)
    scaled = (w * np.exp2(127.0 - byte)[:, None, :]).reshape(k, n).astype(np.float32)
    by_word = np.ascontiguousarray(scaled.reshape(k // 512, 128, 4, n).transpose(0, 1, 3, 2))
    if fmt == "e4m3":
        words = by_word.astype(ml_dtypes.float8_e4m3fn).view(np.uint8)
    else:
        c = by_word.astype(ml_dtypes.float4_e2m1fn).view(np.uint8) & 0xF
        words = (c[..., 0::2] | (c[..., 1::2] << 4)).reshape(k // 512, 128, 2 * n)
    return np.ascontiguousarray(words), np.ascontiguousarray(byte.astype(np.uint8).reshape(k // 512, 16, n))


def unpack_weight(words, scales, fmt):
    g, _, n = scales.shape
    words = np.ascontiguousarray(words).reshape(g, 128, n, -1)
    if fmt == "e4m3":
        vals = words.view(ml_dtypes.float8_e4m3fn).astype(np.float64)
    else:
        nib = np.empty((g, 128, n, 4), np.uint8)
        nib[..., 0::2] = words & 0xF
        nib[..., 1::2] = words >> 4
        vals = E2M1[nib]
    vals = vals * np.repeat(np.exp2(scales.astype(np.float64) - 127.0), 8, axis=1)[..., None]
    return vals.transpose(0, 1, 3, 2).reshape(g * 512, n)


def gelu(v):
    return 0.5 * v * (1.0 + np.tanh(np.sqrt(2.0 / np.pi) * (v + 0.044715 * v**3)))


K, H, T, S, T3, S2, P = 1024, 1024, 2048, 1024, 2048, 512, 512

def setup_inputs():
    n = np.random.standard_normal
    s = mx_kscale(K)[:, None]
    u = mx_kscale(H)[:, None]
    tab_words, tab_scales = pack_weight(n((K, T)) * s, "e4m3")
    tab2_words, tab2_scales = pack_weight(n((H, T3)) / np.sqrt(H) / u, "e4m3")
    w1_words, w1_scales = pack_weight(0.34 * n((K, H)) / np.sqrt(K) / s, "e2m1")
    w2 = (0.75 * n((K, H)) / np.sqrt(K) / s).astype(np.float32)
    return {
        "tab_words": tab_words, "tab_scales": tab_scales,
        "tab2_words": tab2_words, "tab2_scales": tab2_scales,
        "w1_words": w1_words, "w1_scales": w1_scales, "w2": w2,
        "season": np.random.uniform(-1.2, 1.2, (H, S)).astype(np.float32),
        "gain": (np.random.uniform(0.6, 1.5, H) * u[:, 0]).astype(np.float32),
        "scale": np.random.uniform(0.4, 1.6, S2).astype(np.float32),
        "bias": (0.5 * n(S2)).astype(np.float32),
        "lim": n((S2, P)).astype(np.float32),
        "offs": striped(np.random.permutation(T)[:S]),
        "offs2": striped(np.random.permutation(T3)[:S2]),
        "pos1": striped(np.random.permutation(S)[:P]),
        "pos2": striped(np.random.permutation(S)[:P]),
    }

def reference(tab_words, tab_scales, tab2_words, tab2_scales, w1_words, w1_scales, w2, season, gain, scale, bias, lim, offs, offs2, pos1, pos2):
    v = unpack_weight(tab_words, tab_scales, "e4m3")[:, unstriped(offs)]
    v2 = unpack_weight(tab2_words, tab2_scales, "e4m3")[:, unstriped(offs2)]
    w1 = unpack_weight(w1_words, w1_scales, "e2m1")
    wave = np.sin((w1.T @ v) + f64(season))
    plain = mxq(f64(w2), 0, "e4m3").T @ v
    h = f64(gain)[:, None] * np.minimum(wave, plain)
    e = v2.T @ mxq(h, 0, "e4m3")
    a = np.exp(f64(scale)[:, None] * e[:, unstriped(pos1)] + f64(bias)[:, None])
    c = e[:, unstriped(pos2)]
    return np.minimum(a * c, f64(lim))

@@ -1,0 +1,341 @@
+import math
+from contextlib import ExitStack
+
+import concourse.mybir as mybir
+
+K, H, T, S, T3, S2, NP = 1024, 1024, 2048, 1024, 2048, 512, 512
+FLOPS = 2 * (2 * K * H * S + H * S2 * S)
+
+F32 = mybir.dt.float32
+BF16 = mybir.dt.bfloat16
+I32 = mybir.dt.int32
+U32 = mybir.dt.uint32
+U16 = mybir.dt.uint16
+U8 = mybir.dt.uint8
+FP8X4 = mybir.dt.float8_e4m3fn_x4
+FP4X4 = mybir.dt.float4_e2m1fn_x4
+ACT = mybir.ActivationFunctionType
+ALU = mybir.AluOpType
+
+P = 128
+PACK = 4
+K_PASS = P * PACK
+PASSES = K // K_PASS
+HALVES = H // K_PASS
+CHUNK = 128
+SLICE = 256
+SLICES = S // SLICE
+LIST_COLS = SLICE // 16
+M_TILES = S2 // P
+QUADS = 4
+LAG = 2
+
+
+def tile_list_mussel_host_scores_kernel(
+    tc, tab_words, tab_scales, tab2_words, tab2_scales, w1_words, w1_scales, w2, season, gain, scale, bias, lim,
+    offs, offs2, pos1, pos2, out,
+):
+    nc = tc.nc
+    with ExitStack() as ctx:
+        lists = ctx.enter_context(tc.tile_pool(name="lists", bufs=1))
+        keep = ctx.enter_context(tc.tile_pool(name="keep", bufs=1))
+        ring = ctx.enter_context(tc.tile_pool(name="ring", bufs=3))
+        reuse = ctx.enter_context(tc.tile_pool(name="reuse", bufs=1))
+        psum = ctx.enter_context(tc.psum_pool(name="psum", bufs=3))
+        psum_e = ctx.enter_context(tc.psum_pool(name="psum_e", bufs=2))
+
+        def held(name, shape, dtype):
+            return keep.tile(shape, dtype, name=name, align_bytes=64)
+
+        def in_place_of(c, name, shape, dtype, start=0):
+            return reuse.tile(shape, dtype, name=name, align_bytes=64, offset=c * PACK * CHUNK * 4 + start)
+
+        def load_list(name, src):
+            tile = lists.tile(list(src.shape), U16, name=name)
+            nc.sync.dma_start(tile[:], src)
+            return tile
+
+        def load_words(name, src):
+            tile = held(name, [P, src.shape[1]], U32)
+            nc.sync.dma_start(out=tile[:].bitcast(I32), in_=src.rearrange("p t i -> p (t i)").bitcast(I32))
+            return tile
+
+        def load_planes_side_by_side(name, src, clear, queue):
+            width = src.shape[2]
+            tile = held(name, [P, PASSES, width], U8)
+            clear.memset(tile[:].rearrange("p a t -> p (a t)").bitcast(I32), 0)
+            for q in range(QUADS):
+                queue.dma_start(
+                    out=tile[32 * q : 32 * q + 4, :, :].bitcast(I32),
+                    in_=src[:, 4 * q : 4 * q + 4, :].rearrange("a r t -> r a t").bitcast(I32),
+                )
+            return tile
+
+        def load_w2(b, a):
+            tile = keep.tile([P, PACK, K_PASS], F32, name="w2_raw_%d_%d" % (b, a), tag="w2_raw_%d" % a)
+            rows = w2[a * K_PASS : (a + 1) * K_PASS, b * K_PASS : (b + 1) * K_PASS]
+            nc.sync.dma_start(out=tile[:], in_=rows.rearrange("(p i) c -> p i c", i=PACK))
+            return tile
+
+        def load_season(b, s):
+            tile = held("season_%d_%d" % (b, s), [P, PACK, SLICE], F32)
+            rows = season[b * K_PASS : (b + 1) * K_PASS, s * SLICE : (s + 1) * SLICE]
+            nc.sync.dma_start(out=tile[:], in_=rows.rearrange("(p t) j -> p t j", t=PACK))
+            return tile
+
+        idx = load_list("idx", offs)
+        tab_w = [load_words("tab_w%d" % a, tab_words[a]) for a in range(PASSES)]
+        tab_s = load_planes_side_by_side("tab_s", tab_scales, nc.gpsimd, nc.sync)
+        w1_s = load_planes_side_by_side("w1_s", w1_scales, nc.vector, nc.sync)
+        w2_raw = {}
+        season_sb = {}
+        w2_raw[0, 0] = load_w2(0, 0)
+        w1_w = held("w1_w", [P, PASSES, H], U16)
+        nc.sync.dma_start(out=w1_w[:].bitcast(I32), in_=w1_words.rearrange("a p c -> p a c").bitcast(I32))
+        gain_sb = held("gain_sb", [P, HALVES, PACK], F32)
+        nc.sync.dma_start(out=gain_sb[:], in_=gain.rearrange("(b p t) -> p b t", b=HALVES, t=PACK))
+        w2_raw[0, 1] = load_w2(0, 1)
+        for s in range(SLICES):
+            season_sb[0, s] = load_season(0, s)
+        w2_raw[1, 0] = load_w2(1, 0)
+        w2_raw[1, 1] = load_w2(1, 1)
+        season_sb[1, 0] = load_season(1, 0)
+        idx2 = load_list("idx2", offs2)
+        tab2_s = held("tab2_s", [P, T3], U8)
+        nc.vector.memset(tab2_s[:].bitcast(I32), 0)
+        for q in range(QUADS):
+            nc.sync.dma_start(
+                out=tab2_s[32 * q : 32 * q + 4 * HALVES, :].bitcast(I32),
+                in_=tab2_scales[:, 4 * q : 4 * q + 4, :].bitcast(I32),
+            )
+        tab2_w = [load_words("tab2_w%d" % b, tab2_words[b]) for b in range(HALVES)]
+        for s in range(1, SLICES):
+            season_sb[1, s] = load_season(1, s)
+        p1 = load_list("p1", pos1)
+        p2 = load_list("p2", pos2)
+        scale_sb = held("scale_sb", [P, M_TILES], F32)
+        bias_sb = held("bias_sb", [P, M_TILES], F32)
+        with nc.allow_non_contiguous_dma(reason="one value a strain, strains on the partitions"):
+            nc.sync.dma_start(out=scale_sb[:], in_=scale.rearrange("(m p) -> p m", p=P))
+            nc.sync.dma_start(out=bias_sb[:], in_=bias.rearrange("(m p) -> p m", p=P))
+        lim_sb = held("lim_sb", [P, M_TILES, NP], F32)
+        nc.sync.dma_start(out=lim_sb[:], in_=lim.rearrange("(m p) n -> p m n", p=P))
+
+        v_w, v_s = {}, {}
+
+        def gather_scales(s):
+            part = idx[:, s * LIST_COLS : (s + 1) * LIST_COLS]
+            for a in range(PASSES):
+                v_s[a, s] = held("v_s_%d_%d" % (a, s), [P, SLICE], U8)
+                nc.vector.tensor_copy(v_s[a, s][:], tab_s[:, a, :].indirect(part))
+
+        def gather_words(a, s):
+            part = idx[:, s * LIST_COLS : (s + 1) * LIST_COLS]
+            v_w[a, s] = held("v_w_%d_%d" % (a, s), [P, SLICE], U32)
+            nc.vector.tensor_copy(v_w[a, s][:], tab_w[a][:].indirect(part))
+
+        w1_wp, w1_sp = {}, {}
+
+        def deal_w1(b):
+            cols = slice(b * K_PASS, (b + 1) * K_PASS)
+            w1_sp[b] = held("w1_sp_%d" % b, [P, PASSES, PACK, P], U8)
+            nc.gpsimd.tensor_copy(out=w1_sp[b][:], in_=w1_s[:, :, cols].rearrange("p a (m t) -> p a t m", t=PACK))
+            w1_wp[b] = held("w1_wp_%d" % b, [P, PASSES, PACK, P], U16)
+            nc.scalar.copy(
+                out=w1_wp[b][:].rearrange("p a t m -> p a m t"),
+                in_=w1_w[:, :, cols].rearrange("p a (m t) -> p a m t", t=PACK),
+            )
+
+        w2_bf, w2_w, w2_s = {}, {}, {}
+
+        def round_w2(b, a):
+            w2_bf[b, a] = ring.tile([P, PACK * K_PASS], BF16, name="w2_bf", align_bytes=64, bufs=2)
+            nc.scalar.copy(
+                out=w2_bf[b, a][:].rearrange("p (t m i) -> p m i t", t=PACK, i=PACK),
+                in_=w2_raw[b, a][:].rearrange("p i (m t) -> p m i t", t=PACK),
+            )
+
+        def quantise_w2(b, a):
+            w2_w[b, a] = held("w2_w_%d_%d" % (b, a), [P, K_PASS], U32)
+            name = "w2_s_%d_%d" % (b, a)
+            w2_s[b, a] = held(name, [P, K_PASS], U8) if b == 0 else in_place_of(3 + 2 * a, name, [P, K_PASS], U8, 1024)
+            nc.vector.quantize_mx(out=w2_w[b, a][:].bitcast(FP8X4), scales=w2_s[b, a][:], in_=w2_bf[b, a][:])
+
+        chunks = [(b, s, u) for b in range(HALVES) for s in range(SLICES) for u in range(SLICE // CHUNK)]
+        two_sin2, low = {}, {}
+        h_w, h_s = {}, {}
+
+        def wave(c):
+            b, s, u = chunks[c]
+            cols = slice(u * CHUNK, (u + 1) * CHUNK)
+            z1 = psum.tile([P, PACK, CHUNK], F32, name="z1")
+            for t in range(PACK):
+                for a in range(PASSES):
+                    nc.tensor.matmul_mx(
+                        out=z1[:, t, :],
+                        lhsT=w1_wp[b][:, a, t, :].bitcast(FP4X4),
+                        lhsT_scale=w1_sp[b][:, a, t, :],
+                        rhs=v_w[a, s][:, cols].bitcast(FP8X4),
+                        rhs_scale=v_s[a, s][:, cols],
+                        start=(a == 0),
+                        stop=(a == PASSES - 1),
+                    )
+            shifted = ring.tile([P, PACK, CHUNK], F32, name="shifted")
+            nc.vector.scalar_tensor_tensor(
+                out=shifted[:], in0=z1[:], scalar=math.pi / 2, in1=season_sb[b, s][:, :, cols], op0=ALU.add, op1=ALU.add
+            )
+            half_sin = ring.tile([P, PACK, CHUNK], F32, name="half_sin")
+            nc.scalar.activation(out=half_sin[:], in_=shifted[:], func=ACT.Sin, scale=0.5)
+            two_sin2[c] = in_place_of(c, "two_sin2_%d" % c, [P, CHUNK, PACK], F32)
+            nc.scalar.activation(
+                out=two_sin2[c][:].rearrange("p (g i) t -> p g t i", i=4),
+                in_=half_sin[:].rearrange("p t (g i) -> p g t i", i=4),
+                func=ACT.Square,
+                scale=math.sqrt(2.0),
+            )
+
+        def lesser(c):
+            b, s, u = chunks[c]
+            cols = slice(u * CHUNK, (u + 1) * CHUNK)
+            z2 = psum.tile([P, PACK, CHUNK], F32, name="z2")
+            for t in range(PACK):
+                for a in range(PASSES):
+                    nc.tensor.matmul_mx(
+                        out=z2[:, t, :],
+                        lhsT=w2_w[b, a][:, t * P : (t + 1) * P].bitcast(FP8X4),
+                        lhsT_scale=w2_s[b, a][:, t * P : (t + 1) * P],
+                        rhs=v_w[a, s][:, cols].bitcast(FP8X4),
+                        rhs_scale=v_s[a, s][:, cols],
+                        start=(a == 0),
+                        stop=(a == PASSES - 1),
+                    )
+            if u == 0:
+                low[b, s] = ring.tile([P, SLICE, PACK], F32, name="low", bufs=2)
+            nc.vector.scalar_tensor_tensor(
+                out=low[b, s][:, cols, :], in0=two_sin2[c][:], scalar=-1.0, in1=z2[:].rearrange("p t n -> p n t"),
+                op0=ALU.add, op1=ALU.min,
+            )
+
+        h_bf = {}
+
+        def apply_gain(g, engine, tag):
+            b, s = divmod(g, SLICES)
+            h_bf[g] = ring.tile([P, SLICE, PACK], BF16, name=tag, align_bytes=64, bufs=1)
+            engine.tensor_tensor(
+                out=h_bf[g][:],
+                in0=low[b, s][:],
+                in1=gain_sb[:, b : b + 1, :].to_broadcast([P, SLICE, PACK]),
+                op=ALU.mult,
+            )
+
+        def quantise_h(g):
+            b, s = divmod(g, SLICES)
+            name = "h_w_%d_%d" % (b, s)
+            after = 2 * g + 3
+            h_w[b, s] = in_place_of(after, name, [P, SLICE], U32) if after < len(chunks) else held(name, [P, SLICE], U32)
+            h_s[b, s] = held("h_s_%d_%d" % (b, s), [P, SLICE], U8)
+            nc.vector.quantize_mx(
+                out=h_w[b, s][:].bitcast(FP8X4),
+                scales=h_s[b, s][:],
+                in_=h_bf[g][:].rearrange("p n t -> p (n t)"),
+            )
+
+        v2 = {}
+
+        def gather_strain_scales():
+            v2["s"] = in_place_of(11, "v2_s", [P, S2], U8, 1024)
+            nc.vector.tensor_copy(v2["s"][:], tab2_s[:].indirect(idx2[:]))
+
+        def gather_strain_words(b):
+            v2[b] = in_place_of(10 + 2 * b, "v2_w%d" % b, [P, S2], U32)
+            nc.vector.tensor_copy(v2[b][:], tab2_w[b][:].indirect(idx2[:]))
+
+        e_sb = [held("e_%d" % m, [P, S], F32) for m in range(M_TILES)]
+
+        def scores(s, tiles, bank, copy):
+            for i, m in enumerate(tiles):
+                rows = slice(m * P, (m + 1) * P)
+                for b in range(HALVES):
+                    nc.tensor.matmul_mx(
+                        out=bank[:, i, :],
+                        lhsT=v2[b][:, rows].bitcast(FP8X4),
+                        lhsT_scale=v2["s"][4 * b : P, rows],
+                        rhs=h_w[b, s][:].bitcast(FP8X4),
+                        rhs_scale=h_s[b, s][:],
+                        start=(b == 0),
+                        stop=(b == HALVES - 1),
+                    )
+            for i, m in enumerate(tiles):
+                copy(out=e_sb[m][:, s * SLICE : (s + 1) * SLICE], in_=bank[:, i, :])
+
+        def scores_in_pairs(s):
+            for first in range(0, M_TILES, 2):
+                bank = psum_e.tile([P, 2, SLICE], F32, name="e_bank")
+                scores(s, [first, first + 1], bank, nc.scalar.copy)
+
+        def finish(m, parts):
+            width = NP // parts
+            result = ring.tile([P, NP], F32, name="result", bufs=4)
+            for part in range(parts):
+                entries = slice(part * width // 16, (part + 1) * width // 16)
+                cols = slice(part * width, (part + 1) * width)
+                look = ring.tile([P, width], F32, name="look", bufs=3)
+                nc.scalar.activation(
+                    out=look[:], in_=e_sb[m][:].indirect(p1[:, entries]), func=ACT.Exp,
+                    bias=bias_sb[:, m : m + 1], scale=scale_sb[:, m : m + 1],
+                )
+                product = ring.tile([P, width], F32, name="product", bufs=2)
+                nc.vector.tensor_tensor(product[:], e_sb[m][:].indirect(p2[:, entries]), look[:], ALU.mult)
+                nc.vector.tensor_tensor(result[:, cols], product[:], lim_sb[:, m, cols], ALU.min)
+            nc.sync.dma_start(out=out[m * P : (m + 1) * P, :], in_=result[:])
+
+        for a in range(PASSES):
+            for s in range(SLICES):
+                gather_words(a, s)
+        gather_scales(0)
+        round_w2(0, 0)
+        deal_w1(0)
+        round_w2(0, 1)
+        gather_scales(1)
+        quantise_w2(0, 0)
+        deal_w1(1)
+        n = len(chunks)
+        for step in range(n + LAG):
+            if step < n:
+                b, s, u = chunks[step]
+                if b == 0 and u == 0 and s + 2 < SLICES:
+                    gather_scales(s + 2)
+                wave(step)
+            if step == 1:
+                quantise_w2(0, 1)
+            if step in (3, 5):
+                round_w2(1, (step - 3) // 2)
+            c = step - LAG
+            if c < 0:
+                continue
+            lesser(c)
+            if c == 10 or c == 12:
+                gather_strain_words((c - 10) // 2)
+            if c % 2 == 1:
+                g = c // 2
+                if c in (3, 5):
+                    quantise_w2(1, (c - 3) // 2)
+                if g > 0:
+                    quantise_h(g - 1)
+                if c < n - 1:
+                    apply_gain(g, nc.gpsimd, "h_bf")
+                else:
+                    apply_gain(g, nc.vector, "h_last")
+                if c == 11:
+                    gather_strain_scales()
+                if c == 13:
+                    scores_in_pairs(0)
+                    scores_in_pairs(1)
+                if c == 15:
+                    scores_in_pairs(2)
+        quantise_h(HALVES * SLICES - 1)
+        for m in range(M_TILES):
+            bank = psum.tile([P, 1, SLICE], F32, name="z1" if m < 2 else "z2")
+            scores(SLICES - 1, [m], bank, nc.vector.tensor_copy)
+        for m in range(M_TILES):
+            finish(m, 2 if m == 0 else 1)

@@ -25,10 +25,19 @@ HALVES = H // K_PASS
 CHUNK = 128
 SLICE = 256
 SLICES = S // SLICE
-LIST_COLS = SLICE // 16
+STEPS = HALVES * SLICES
 M_TILES = S2 // P
 QUADS = 4
-LAG = 2
+
+CHUNK_BYTES = CHUNK * PACK * 4
+LOW_AT = 2 * STEPS * CHUNK_BYTES
+LOW_BYTES = SLICE * PACK * 4
+ROUNDED_BYTES = SLICE * PACK * 2
+ROUNDED_AT = LOW_AT + 3 * LOW_BYTES
+TAB2_S_AT = ROUNDED_AT + ROUNDED_BYTES
+TAB2_W1_AT = TAB2_S_AT + T3
+W2_BF_AT = TAB2_W1_AT + 4 * T3
+TURN = SLICES - 1
 
 
 def tile_list_mussel_host_scores_kernel(
@@ -39,7 +48,7 @@ def tile_list_mussel_host_scores_kernel(
     with ExitStack() as ctx:
         lists = ctx.enter_context(tc.tile_pool(name="lists", bufs=1))
         keep = ctx.enter_context(tc.tile_pool(name="keep", bufs=1))
-        ring = ctx.enter_context(tc.tile_pool(name="ring", bufs=3))
+        ring = ctx.enter_context(tc.tile_pool(name="ring", bufs=2))
         reuse = ctx.enter_context(tc.tile_pool(name="reuse", bufs=1))
         psum = ctx.enter_context(tc.psum_pool(name="psum", bufs=3))
         psum_e = ctx.enter_context(tc.psum_pool(name="psum_e", bufs=2))
@@ -47,70 +56,70 @@ def tile_list_mussel_host_scores_kernel(
         def held(name, shape, dtype):
             return keep.tile(shape, dtype, name=name, align_bytes=64)
 
-        def in_place_of(c, name, shape, dtype, start=0):
-            return reuse.tile(shape, dtype, name=name, align_bytes=64, offset=c * PACK * CHUNK * 4 + start)
+        def placed(name, shape, dtype, offset):
+            return reuse.tile(shape, dtype, name=name, align_bytes=64, offset=offset)
 
         def load_list(name, src):
             tile = lists.tile(list(src.shape), U16, name=name)
             nc.sync.dma_start(tile[:], src)
             return tile
 
-        def load_words(name, src):
-            tile = held(name, [P, src.shape[1]], U32)
+        def load_words(tile, src):
             nc.sync.dma_start(out=tile[:].bitcast(I32), in_=src.rearrange("p t i -> p (t i)").bitcast(I32))
             return tile
 
-        def load_planes_side_by_side(name, src, clear, queue):
-            width = src.shape[2]
-            tile = held(name, [P, PASSES, width], U8)
+        def load_planes_side_by_side(name, src, clear):
+            tile = held(name, [P, PASSES, src.shape[2]], U8)
             clear.memset(tile[:].rearrange("p a t -> p (a t)").bitcast(I32), 0)
             for q in range(QUADS):
-                queue.dma_start(
+                nc.sync.dma_start(
                     out=tile[32 * q : 32 * q + 4, :, :].bitcast(I32),
                     in_=src[:, 4 * q : 4 * q + 4, :].rearrange("a r t -> r a t").bitcast(I32),
                 )
             return tile
 
-        def load_w2(b, a):
-            tile = keep.tile([P, PACK, K_PASS], F32, name="w2_raw_%d_%d" % (b, a), tag="w2_raw_%d" % a)
-            rows = w2[a * K_PASS : (a + 1) * K_PASS, b * K_PASS : (b + 1) * K_PASS]
-            nc.sync.dma_start(out=tile[:], in_=rows.rearrange("(p i) c -> p i c", i=PACK))
-            return tile
+        w2_raw, season_sb = {}, {}
 
-        def load_season(b, s):
-            tile = held("season_%d_%d" % (b, s), [P, PACK, SLICE], F32)
+        def load_w2(b, a):
+            w2_raw[b, a] = keep.tile([P, PACK, K_PASS], F32, name="w2_raw_%d_%d" % (b, a), tag="w2_raw_%d" % a)
+            rows = w2[a * K_PASS : (a + 1) * K_PASS, b * K_PASS : (b + 1) * K_PASS]
+            nc.sync.dma_start(out=w2_raw[b, a][:], in_=rows.rearrange("(p i) c -> p i c", i=PACK))
+
+        def load_season(g):
+            b, s = divmod(g, SLICES)
+            season_sb[g] = held("season_%d" % g, [P, PACK, SLICE], F32)
             rows = season[b * K_PASS : (b + 1) * K_PASS, s * SLICE : (s + 1) * SLICE]
-            nc.sync.dma_start(out=tile[:], in_=rows.rearrange("(p t) j -> p t j", t=PACK))
-            return tile
+            nc.sync.dma_start(out=season_sb[g][:], in_=rows.rearrange("(p t) j -> p t j", t=PACK))
 
         idx = load_list("idx", offs)
-        tab_w = [load_words("tab_w%d" % a, tab_words[a]) for a in range(PASSES)]
-        tab_s = load_planes_side_by_side("tab_s", tab_scales, nc.gpsimd, nc.sync)
-        w1_s = load_planes_side_by_side("w1_s", w1_scales, nc.vector, nc.sync)
-        w2_raw = {}
-        season_sb = {}
-        w2_raw[0, 0] = load_w2(0, 0)
+        w1_s = load_planes_side_by_side("w1_s", w1_scales, nc.gpsimd)
+        tab_w = [load_words(held("tab_w%d" % a, [P, T], U32), tab_words[a]) for a in range(PASSES)]
         w1_w = held("w1_w", [P, PASSES, H], U16)
         nc.sync.dma_start(out=w1_w[:].bitcast(I32), in_=w1_words.rearrange("a p c -> p a c").bitcast(I32))
+        tab_s = load_planes_side_by_side("tab_s", tab_scales, nc.vector)
+        load_w2(0, 0)
+        load_w2(0, 1)
+        load_season(0)
         gain_sb = held("gain_sb", [P, HALVES, PACK], F32)
         nc.sync.dma_start(out=gain_sb[:], in_=gain.rearrange("(b p t) -> p b t", b=HALVES, t=PACK))
-        w2_raw[0, 1] = load_w2(0, 1)
-        for s in range(SLICES):
-            season_sb[0, s] = load_season(0, s)
-        w2_raw[1, 0] = load_w2(1, 0)
-        w2_raw[1, 1] = load_w2(1, 1)
-        season_sb[1, 0] = load_season(1, 0)
+        for g in range(1, SLICES):
+            load_season(g)
+        load_w2(1, 0)
         idx2 = load_list("idx2", offs2)
-        tab2_s = held("tab2_s", [P, T3], U8)
-        nc.vector.memset(tab2_s[:].bitcast(I32), 0)
+        tab2_s = placed("tab2_s", [P, T3], U8, TAB2_S_AT)
+        nc.gpsimd.memset(tab2_s[:].bitcast(I32), 0)
         for q in range(QUADS):
             nc.sync.dma_start(
                 out=tab2_s[32 * q : 32 * q + 4 * HALVES, :].bitcast(I32),
                 in_=tab2_scales[:, 4 * q : 4 * q + 4, :].bitcast(I32),
             )
-        tab2_w = [load_words("tab2_w%d" % b, tab2_words[b]) for b in range(HALVES)]
-        for s in range(1, SLICES):
-            season_sb[1, s] = load_season(1, s)
+        tab2_w = [
+            load_words(held("tab2_w0", [P, T3], U32), tab2_words[0]),
+            load_words(placed("tab2_w1", [P, T3], U32, TAB2_W1_AT), tab2_words[1]),
+        ]
+        load_w2(1, 1)
+        for g in range(SLICES, STEPS):
+            load_season(g)
         p1 = load_list("p1", pos1)
         p2 = load_list("p2", pos2)
         scale_sb = held("scale_sb", [P, M_TILES], F32)
@@ -118,28 +127,27 @@ def tile_list_mussel_host_scores_kernel(
         with nc.allow_non_contiguous_dma(reason="one value a strain, strains on the partitions"):
             nc.sync.dma_start(out=scale_sb[:], in_=scale.rearrange("(m p) -> p m", p=P))
             nc.sync.dma_start(out=bias_sb[:], in_=bias.rearrange("(m p) -> p m", p=P))
-        lim_sb = held("lim_sb", [P, M_TILES, NP], F32)
+        lim_sb = keep.tile([P, M_TILES, NP], F32, name="lim_sb", tag="w2_raw_0")
         nc.sync.dma_start(out=lim_sb[:], in_=lim.rearrange("(m p) n -> p m n", p=P))
 
-        v_w, v_s = {}, {}
+        v_w = [held("v_w%d" % a, [P, S], U32) for a in range(PASSES)]
+        v_s = [held("v_s%d" % a, [P, S], U8) for a in range(PASSES)]
 
-        def gather_scales(s):
-            part = idx[:, s * LIST_COLS : (s + 1) * LIST_COLS]
-            for a in range(PASSES):
-                v_s[a, s] = held("v_s_%d_%d" % (a, s), [P, SLICE], U8)
-                nc.vector.tensor_copy(v_s[a, s][:], tab_s[:, a, :].indirect(part))
+        def gather_scales(a, first, last):
+            nc.vector.tensor_copy(v_s[a][:, first:last], tab_s[:, a, :].indirect(idx[:, first // 16 : last // 16]))
 
-        def gather_words(a, s):
-            part = idx[:, s * LIST_COLS : (s + 1) * LIST_COLS]
-            v_w[a, s] = held("v_w_%d_%d" % (a, s), [P, SLICE], U32)
-            nc.vector.tensor_copy(v_w[a, s][:], tab_w[a][:].indirect(part))
+        def gather_words(a, first, last):
+            nc.vector.tensor_copy(v_w[a][:, first:last], tab_w[a][:].indirect(idx[:, first // 16 : last // 16]))
 
         w1_wp, w1_sp = {}, {}
 
-        def deal_w1(b):
+        def deal_w1_scales(b):
             cols = slice(b * K_PASS, (b + 1) * K_PASS)
             w1_sp[b] = held("w1_sp_%d" % b, [P, PASSES, PACK, P], U8)
-            nc.gpsimd.tensor_copy(out=w1_sp[b][:], in_=w1_s[:, :, cols].rearrange("p a (m t) -> p a t m", t=PACK))
+            nc.vector.tensor_copy(out=w1_sp[b][:], in_=w1_s[:, :, cols].rearrange("p a (m t) -> p a t m", t=PACK))
+
+        def deal_w1_words(b):
+            cols = slice(b * K_PASS, (b + 1) * K_PASS)
             w1_wp[b] = held("w1_wp_%d" % b, [P, PASSES, PACK, P], U16)
             nc.scalar.copy(
                 out=w1_wp[b][:].rearrange("p a t m -> p a m t"),
@@ -149,7 +157,10 @@ def tile_list_mussel_host_scores_kernel(
         w2_bf, w2_w, w2_s = {}, {}, {}
 
         def round_w2(b, a):
-            w2_bf[b, a] = ring.tile([P, PACK * K_PASS], BF16, name="w2_bf", align_bytes=64, bufs=2)
+            if (b, a) == (1, 1):
+                w2_bf[b, a] = placed("w2_bf_last", [P, PACK * K_PASS], BF16, W2_BF_AT)
+            else:
+                w2_bf[b, a] = ring.tile([P, PACK * K_PASS], BF16, name="w2_bf", align_bytes=64)
             nc.scalar.copy(
                 out=w2_bf[b, a][:].rearrange("p (t m i) -> p m i t", t=PACK, i=PACK),
                 in_=w2_raw[b, a][:].rearrange("p i (m t) -> p m i t", t=PACK),
@@ -158,124 +169,135 @@ def tile_list_mussel_host_scores_kernel(
         def quantise_w2(b, a):
             w2_w[b, a] = held("w2_w_%d_%d" % (b, a), [P, K_PASS], U32)
             name = "w2_s_%d_%d" % (b, a)
-            w2_s[b, a] = held(name, [P, K_PASS], U8) if b == 0 else in_place_of(3 + 2 * a, name, [P, K_PASS], U8, 1024)
+            if b == 0:
+                w2_s[b, a] = held(name, [P, K_PASS], U8)
+            else:
+                w2_s[b, a] = placed(name, [P, K_PASS], U8, TAB2_W1_AT if a == 1 else TAB2_S_AT)
             nc.vector.quantize_mx(out=w2_w[b, a][:].bitcast(FP8X4), scales=w2_s[b, a][:], in_=w2_bf[b, a][:])
 
-        chunks = [(b, s, u) for b in range(HALVES) for s in range(SLICES) for u in range(SLICE // CHUNK)]
-        two_sin2, low = {}, {}
-        h_w, h_s = {}, {}
+        two_sin2, low, h_bf, h_w, h_s = {}, {}, {}, {}, {}
 
-        def wave(c):
-            b, s, u = chunks[c]
-            cols = slice(u * CHUNK, (u + 1) * CHUNK)
-            z1 = psum.tile([P, PACK, CHUNK], F32, name="z1")
-            for t in range(PACK):
-                for a in range(PASSES):
-                    nc.tensor.matmul_mx(
-                        out=z1[:, t, :],
-                        lhsT=w1_wp[b][:, a, t, :].bitcast(FP4X4),
-                        lhsT_scale=w1_sp[b][:, a, t, :],
-                        rhs=v_w[a, s][:, cols].bitcast(FP8X4),
-                        rhs_scale=v_s[a, s][:, cols],
-                        start=(a == 0),
-                        stop=(a == PASSES - 1),
-                    )
-            shifted = ring.tile([P, PACK, CHUNK], F32, name="shifted")
-            nc.vector.scalar_tensor_tensor(
-                out=shifted[:], in0=z1[:], scalar=math.pi / 2, in1=season_sb[b, s][:, :, cols], op0=ALU.add, op1=ALU.add
-            )
-            half_sin = ring.tile([P, PACK, CHUNK], F32, name="half_sin")
-            nc.scalar.activation(out=half_sin[:], in_=shifted[:], func=ACT.Sin, scale=0.5)
-            two_sin2[c] = in_place_of(c, "two_sin2_%d" % c, [P, CHUNK, PACK], F32)
-            nc.scalar.activation(
-                out=two_sin2[c][:].rearrange("p (g i) t -> p g t i", i=4),
-                in_=half_sin[:].rearrange("p t (g i) -> p g t i", i=4),
-                func=ACT.Square,
-                scale=math.sqrt(2.0),
-            )
-
-        def lesser(c):
-            b, s, u = chunks[c]
-            cols = slice(u * CHUNK, (u + 1) * CHUNK)
-            z2 = psum.tile([P, PACK, CHUNK], F32, name="z2")
-            for t in range(PACK):
-                for a in range(PASSES):
-                    nc.tensor.matmul_mx(
-                        out=z2[:, t, :],
-                        lhsT=w2_w[b, a][:, t * P : (t + 1) * P].bitcast(FP8X4),
-                        lhsT_scale=w2_s[b, a][:, t * P : (t + 1) * P],
-                        rhs=v_w[a, s][:, cols].bitcast(FP8X4),
-                        rhs_scale=v_s[a, s][:, cols],
-                        start=(a == 0),
-                        stop=(a == PASSES - 1),
-                    )
-            if u == 0:
-                low[b, s] = ring.tile([P, SLICE, PACK], F32, name="low", bufs=2)
-            nc.vector.scalar_tensor_tensor(
-                out=low[b, s][:, cols, :], in0=two_sin2[c][:], scalar=-1.0, in1=z2[:].rearrange("p t n -> p n t"),
-                op0=ALU.add, op1=ALU.min,
-            )
-
-        h_bf = {}
-
-        def apply_gain(g, engine, tag):
+        def wave(g):
             b, s = divmod(g, SLICES)
-            h_bf[g] = ring.tile([P, SLICE, PACK], BF16, name=tag, align_bytes=64, bufs=1)
+            cols = slice(s * SLICE, (s + 1) * SLICE)
+            shifted = ring.tile([P, PACK, SLICE], F32, name="shifted")
+            half_sin = ring.tile([P, PACK, SLICE], F32, name="half_sin")
+            for pair in range(PACK // 2):
+                ts = slice(2 * pair, 2 * pair + 2)
+                z1 = psum.tile([P, 2, SLICE], F32, name="z1")
+                for i in range(2):
+                    for a in range(PASSES):
+                        nc.tensor.matmul_mx(
+                            out=z1[:, i, :],
+                            lhsT=w1_wp[b][:, a, 2 * pair + i, :].bitcast(FP4X4),
+                            lhsT_scale=w1_sp[b][:, a, 2 * pair + i, :],
+                            rhs=v_w[a][:, cols].bitcast(FP8X4),
+                            rhs_scale=v_s[a][:, cols],
+                            start=(a == 0),
+                            stop=(a == PASSES - 1),
+                        )
+                nc.vector.scalar_tensor_tensor(
+                    out=shifted[:, ts, :], in0=z1[:], scalar=math.pi / 2, in1=season_sb[g][:, ts, :],
+                    op0=ALU.add, op1=ALU.add,
+                )
+                nc.scalar.activation(out=half_sin[:, ts, :], in_=shifted[:, ts, :], func=ACT.Sin, scale=0.5)
+            for u in range(SLICE // CHUNK):
+                c = 2 * g + u
+                two_sin2[c] = placed("two_sin2_%d" % c, [P, CHUNK, PACK], F32, c * CHUNK_BYTES)
+                nc.scalar.activation(
+                    out=two_sin2[c][:].rearrange("p (n i) t -> p n t i", i=4),
+                    in_=half_sin[:, :, u * CHUNK : (u + 1) * CHUNK].rearrange("p t (n i) -> p n t i", i=4),
+                    func=ACT.Square,
+                    scale=math.sqrt(2.0),
+                )
+
+        def low_at(g):
+            slot = 2 if g % 2 == 0 and g > TURN else g % 2
+            return LOW_AT + slot * LOW_BYTES
+
+        def lesser(g):
+            b, s = divmod(g, SLICES)
+            low[g] = placed("low_%d" % g, [P, SLICE, PACK], F32, low_at(g))
+            for u in range(SLICE // CHUNK):
+                cols = slice(s * SLICE + u * CHUNK, s * SLICE + (u + 1) * CHUNK)
+                z2 = psum.tile([P, PACK, CHUNK], F32, name="z2")
+                for t in range(PACK):
+                    for a in range(PASSES):
+                        nc.tensor.matmul_mx(
+                            out=z2[:, t, :],
+                            lhsT=w2_w[b, a][:, t * P : (t + 1) * P].bitcast(FP8X4),
+                            lhsT_scale=w2_s[b, a][:, t * P : (t + 1) * P],
+                            rhs=v_w[a][:, cols].bitcast(FP8X4),
+                            rhs_scale=v_s[a][:, cols],
+                            start=(a == 0),
+                            stop=(a == PASSES - 1),
+                        )
+                nc.vector.scalar_tensor_tensor(
+                    out=low[g][:, u * CHUNK : (u + 1) * CHUNK, :], in0=two_sin2[2 * g + u][:], scalar=-1.0,
+                    in1=z2[:].rearrange("p t n -> p n t"), op0=ALU.add, op1=ALU.min,
+                )
+
+        def apply_gain(g):
+            b = g // SLICES
+            if g == STEPS - 1:
+                h_bf[g] = held("h_bf_last", [P, SLICE, PACK], BF16)
+            else:
+                h_bf[g] = placed("h_bf_%d" % g, [P, SLICE, PACK], BF16, ROUNDED_AT)
+            engine = nc.vector if g == STEPS - 1 else nc.gpsimd
             engine.tensor_tensor(
                 out=h_bf[g][:],
-                in0=low[b, s][:],
+                in0=low[g][:],
                 in1=gain_sb[:, b : b + 1, :].to_broadcast([P, SLICE, PACK]),
                 op=ALU.mult,
             )
 
         def quantise_h(g):
-            b, s = divmod(g, SLICES)
-            name = "h_w_%d_%d" % (b, s)
-            after = 2 * g + 3
-            h_w[b, s] = in_place_of(after, name, [P, SLICE], U32) if after < len(chunks) else held(name, [P, SLICE], U32)
-            h_s[b, s] = held("h_s_%d_%d" % (b, s), [P, SLICE], U8)
+            if g + 1 < STEPS:
+                h_w[g] = placed("h_w_%d" % g, [P, SLICE], U32, (2 * g + 3) * CHUNK_BYTES)
+            else:
+                h_w[g] = held("h_w_last", [P, SLICE], U32)
+            if g == TURN - 1:
+                h_s[g] = placed("h_s_%d" % g, [P, SLICE], U8, W2_BF_AT)
+            else:
+                h_s[g] = held("h_s_%d" % g, [P, SLICE], U8)
             nc.vector.quantize_mx(
-                out=h_w[b, s][:].bitcast(FP8X4),
-                scales=h_s[b, s][:],
-                in_=h_bf[g][:].rearrange("p n t -> p (n t)"),
+                out=h_w[g][:].bitcast(FP8X4), scales=h_s[g][:], in_=h_bf[g][:].rearrange("p n t -> p (n t)")
             )
 
-        v2 = {}
+        v2_w = {}
+        v2_s = {}
 
-        def gather_strain_scales():
-            v2["s"] = in_place_of(11, "v2_s", [P, S2], U8, 1024)
-            nc.vector.tensor_copy(v2["s"][:], tab2_s[:].indirect(idx2[:]))
-
-        def gather_strain_words(b):
-            v2[b] = in_place_of(10 + 2 * b, "v2_w%d" % b, [P, S2], U32)
-            nc.vector.tensor_copy(v2[b][:], tab2_w[b][:].indirect(idx2[:]))
+        def gather_strains():
+            v2_s[0] = placed("v2_s", [P, S2], U8, (2 * TURN + 1) * CHUNK_BYTES + 4 * SLICE)
+            nc.vector.tensor_copy(v2_s[0][:], tab2_s[:].indirect(idx2[:]))
+            for b in range(HALVES):
+                v2_w[b] = placed("v2_w%d" % b, [P, S2], U32, low_at(TURN - 1) + b * 4 * S2)
+                nc.vector.tensor_copy(v2_w[b][:], tab2_w[b][:].indirect(idx2[:]))
 
         e_sb = [held("e_%d" % m, [P, S], F32) for m in range(M_TILES)]
 
-        def scores(s, tiles, bank, copy):
-            for i, m in enumerate(tiles):
-                rows = slice(m * P, (m + 1) * P)
-                for b in range(HALVES):
-                    nc.tensor.matmul_mx(
-                        out=bank[:, i, :],
-                        lhsT=v2[b][:, rows].bitcast(FP8X4),
-                        lhsT_scale=v2["s"][4 * b : P, rows],
-                        rhs=h_w[b, s][:].bitcast(FP8X4),
-                        rhs_scale=h_s[b, s][:],
-                        start=(b == 0),
-                        stop=(b == HALVES - 1),
-                    )
-            for i, m in enumerate(tiles):
-                copy(out=e_sb[m][:, s * SLICE : (s + 1) * SLICE], in_=bank[:, i, :])
+        def multiply_scores(m, s, sums):
+            rows = slice(m * P, (m + 1) * P)
+            for b in range(HALVES):
+                nc.tensor.matmul_mx(
+                    out=sums,
+                    lhsT=v2_w[b][:, rows].bitcast(FP8X4),
+                    lhsT_scale=v2_s[0][4 * b : P, rows],
+                    rhs=h_w[b * SLICES + s][:].bitcast(FP8X4),
+                    rhs_scale=h_s[b * SLICES + s][:],
+                    start=(b == 0),
+                    stop=(b == HALVES - 1),
+                )
 
-        def scores_in_pairs(s):
-            for first in range(0, M_TILES, 2):
-                bank = psum_e.tile([P, 2, SLICE], F32, name="e_bank")
-                scores(s, [first, first + 1], bank, nc.scalar.copy)
+        def scores(s, tiles):
+            bank = psum_e.tile([P, len(tiles), SLICE], F32, name="e_bank")
+            for i, m in enumerate(tiles):
+                multiply_scores(m, s, bank[:, i, :])
+            for i, m in enumerate(tiles):
+                nc.scalar.copy(out=e_sb[m][:, s * SLICE : (s + 1) * SLICE], in_=bank[:, i, :])
 
         def finish(m, parts):
             width = NP // parts
-            result = ring.tile([P, NP], F32, name="result", bufs=4)
             for part in range(parts):
                 entries = slice(part * width // 16, (part + 1) * width // 16)
                 cols = slice(part * width, (part + 1) * width)
@@ -284,58 +306,54 @@ def tile_list_mussel_host_scores_kernel(
                     out=look[:], in_=e_sb[m][:].indirect(p1[:, entries]), func=ACT.Exp,
                     bias=bias_sb[:, m : m + 1], scale=scale_sb[:, m : m + 1],
                 )
-                product = ring.tile([P, width], F32, name="product", bufs=2)
+                product = ring.tile([P, width], F32, name="product")
                 nc.vector.tensor_tensor(product[:], e_sb[m][:].indirect(p2[:, entries]), look[:], ALU.mult)
-                nc.vector.tensor_tensor(result[:, cols], product[:], lim_sb[:, m, cols], ALU.min)
-            nc.sync.dma_start(out=out[m * P : (m + 1) * P, :], in_=result[:])
+                result = ring.tile([P, width], F32, name="result", bufs=4)
+                nc.vector.tensor_tensor(result[:], product[:], lim_sb[:, m, cols], ALU.min)
+                nc.sync.dma_start(out=out[m * P : (m + 1) * P, cols], in_=result[:])
 
+        for b in range(HALVES):
+            deal_w1_scales(b)
+        gather_words(0, 0, S)
+        gather_words(1, 0, S)
         for a in range(PASSES):
-            for s in range(SLICES):
-                gather_words(a, s)
-        gather_scales(0)
-        round_w2(0, 0)
-        deal_w1(0)
-        round_w2(0, 1)
-        gather_scales(1)
+            gather_scales(a, 0, SLICE)
+        for b in range(HALVES):
+            deal_w1_words(b)
+        for a in range(PASSES):
+            round_w2(0, a)
         quantise_w2(0, 0)
-        deal_w1(1)
-        n = len(chunks)
-        for step in range(n + LAG):
-            if step < n:
-                b, s, u = chunks[step]
-                if b == 0 and u == 0 and s + 2 < SLICES:
-                    gather_scales(s + 2)
-                wave(step)
-            if step == 1:
-                quantise_w2(0, 1)
-            if step in (3, 5):
-                round_w2(1, (step - 3) // 2)
-            c = step - LAG
-            if c < 0:
-                continue
-            lesser(c)
-            if c == 10 or c == 12:
-                gather_strain_words((c - 10) // 2)
-            if c % 2 == 1:
-                g = c // 2
-                if c in (3, 5):
-                    quantise_w2(1, (c - 3) // 2)
-                if g > 0:
-                    quantise_h(g - 1)
-                if c < n - 1:
-                    apply_gain(g, nc.gpsimd, "h_bf")
-                else:
-                    apply_gain(g, nc.vector, "h_last")
-                if c == 11:
-                    gather_strain_scales()
-                if c == 13:
-                    scores_in_pairs(0)
-                    scores_in_pairs(1)
-                if c == 15:
-                    scores_in_pairs(2)
-        quantise_h(HALVES * SLICES - 1)
-        for m in range(M_TILES):
-            bank = psum.tile([P, 1, SLICE], F32, name="z1" if m < 2 else "z2")
-            scores(SLICES - 1, [m], bank, nc.vector.tensor_copy)
-        for m in range(M_TILES):
-            finish(m, 2 if m == 0 else 1)
+        wave(0)
+        gather_scales(0, SLICE, S)
+        quantise_w2(0, 1)
+        gather_scales(1, SLICE, S)
+        for g in range(STEPS):
+            if 0 <= g - (TURN - 1) < PASSES:
+                round_w2(1, g - (TURN - 1))
+            if g + 1 < STEPS:
+                wave(g + 1)
+            lesser(g)
+            if g == TURN:
+                gather_strains()
+                for a in range(PASSES):
+                    quantise_w2(1, a)
+            if g > 0:
+                quantise_h(g - 1)
+            apply_gain(g)
+            if SLICES < g < STEPS - 1:
+                for first in range(0, M_TILES, 2):
+                    scores(g - 1 - SLICES, [first, first + 1])
+        scores(SLICES - 2, [0])
+        last_two = [psum.tile([P, 2, SLICE], F32, name="z1") for m in range(1, M_TILES)]
+        for m in range(1, M_TILES):
+            multiply_scores(m, SLICES - 2, last_two[m - 1][:, 0, :])
+        quantise_h(STEPS - 1)
+        first_bank = psum_e.tile([P, SLICE], F32, name="e_bank")
+        multiply_scores(0, SLICES - 1, first_bank[:])
+        nc.vector.tensor_copy(out=e_sb[0][:, S - SLICE :], in_=first_bank[:])
+        for m in range(1, M_TILES):
+            multiply_scores(m, SLICES - 1, last_two[m - 1][:, 1, :])
+        finish(0, 2)
+        for m in range(1, M_TILES):
+            nc.scalar.copy(out=e_sb[m][:, S - 2 * SLICE :], in_=last_two[m - 1][:].rearrange("p s j -> p (s j)"))
+            finish(m, 2 if m == M_TILES - 1 else 1)

@@ -32,12 +32,10 @@ QUADS = 4
 CHUNK_BYTES = CHUNK * PACK * 4
 LOW_AT = 2 * STEPS * CHUNK_BYTES
 LOW_BYTES = SLICE * PACK * 4
-ROUNDED_BYTES = SLICE * PACK * 2
-ROUNDED_AT = LOW_AT + 3 * LOW_BYTES
-TAB2_S_AT = ROUNDED_AT + ROUNDED_BYTES
-TAB2_W1_AT = TAB2_S_AT + T3
-W2_BF_AT = TAB2_W1_AT + 4 * T3
+W2_BF_AT = LOW_AT + 2 * LOW_BYTES
+STRIP = 64
 TURN = SLICES - 1
+MOVED_ROWS = 112
 
 
 def tile_list_mussel_host_scores_kernel(
@@ -78,6 +76,15 @@ def tile_list_mussel_host_scores_kernel(
                 )
             return tile
 
+        def load_planes_packed(name, src):
+            tile = held(name, [P, src.shape[2]], U8)
+            nc.vector.memset(tile[:].bitcast(I32), 0)
+            for q in range(QUADS):
+                nc.sync.dma_start(
+                    out=tile[32 * q : 32 * q + 8, :].bitcast(I32), in_=src[:, 4 * q : 4 * q + 4, :].bitcast(I32)
+                )
+            return tile
+
         w2_raw, season_sb = {}, {}
 
         def load_w2(b, a):
@@ -92,33 +99,56 @@ def tile_list_mussel_host_scores_kernel(
             nc.sync.dma_start(out=season_sb[g][:], in_=rows.rearrange("(p t) j -> p t j", t=PACK))
 
         idx = load_list("idx", offs)
-        w1_s = load_planes_side_by_side("w1_s", w1_scales, nc.gpsimd)
+        w1_s = load_planes_side_by_side("w1_s", w1_scales, nc.vector)
         tab_w = [load_words(held("tab_w%d" % a, [P, T], U32), tab_words[a]) for a in range(PASSES)]
         w1_w = held("w1_w", [P, PASSES, H], U16)
         nc.sync.dma_start(out=w1_w[:].bitcast(I32), in_=w1_words.rearrange("a p c -> p a c").bitcast(I32))
-        tab_s = load_planes_side_by_side("tab_s", tab_scales, nc.vector)
+        tab_s = load_planes_packed("tab_s", tab_scales)
         load_w2(0, 0)
-        load_w2(0, 1)
         load_season(0)
+
+        w1_wp, w1_sp = {}, {}
+
+        def deal_w1_scales(b):
+            cols = slice(b * K_PASS, (b + 1) * K_PASS)
+            w1_sp[b] = held("w1_sp_%d" % b, [P, PASSES, PACK, P], U8)
+            nc.vector.tensor_copy(out=w1_sp[b][:], in_=w1_s[:, :, cols].rearrange("p a (m t) -> p a t m", t=PACK))
+
+        v_w = {}
+        v_s = held("v_s", [P, S], U8)
+        v_s_low = held("v_s_low", [P, S], U8)
+        nc.vector.memset(v_s_low[96:P, :].bitcast(I32), 0)
+
+        def gather_scales(first, last):
+            nc.vector.tensor_copy(v_s[:, first:last], tab_s[:].indirect(idx[:, first // 16 : last // 16]))
+            nc.sync.dma_start(
+                out=v_s_low[0:MOVED_ROWS, first:last].bitcast(I32), in_=v_s[4 : 4 + MOVED_ROWS, first:last].bitcast(I32)
+            )
+
+        def gather_words(a, tile, first, last):
+            nc.vector.tensor_copy(tile[:], tab_w[a][:].indirect(idx[:, first // 16 : last // 16]))
+            for s in range(first // SLICE, last // SLICE):
+                v_w[a, s] = tile[:, s * SLICE - first : (s + 1) * SLICE - first]
+
+        for b in range(HALVES):
+            deal_w1_scales(b)
+        gather_words(0, held("v_w0", [P, S], U32), 0, S)
+        gather_words(1, held("v_w1", [P, S - SLICE], U32), 0, S - SLICE)
+        gather_scales(0, SLICE)
+        load_w2(0, 1)
+        gather_scales(SLICE, S)
+        load_season(1)
         gain_sb = held("gain_sb", [P, HALVES, PACK], F32)
         nc.sync.dma_start(out=gain_sb[:], in_=gain.rearrange("(b p t) -> p b t", b=HALVES, t=PACK))
-        for g in range(1, SLICES):
+        for g in range(2, SLICES):
             load_season(g)
         load_w2(1, 0)
         idx2 = load_list("idx2", offs2)
-        tab2_s = placed("tab2_s", [P, T3], U8, TAB2_S_AT)
-        nc.gpsimd.memset(tab2_s[:].bitcast(I32), 0)
-        for q in range(QUADS):
-            nc.sync.dma_start(
-                out=tab2_s[32 * q : 32 * q + 4 * HALVES, :].bitcast(I32),
-                in_=tab2_scales[:, 4 * q : 4 * q + 4, :].bitcast(I32),
-            )
-        tab2_w = [
-            load_words(held("tab2_w0", [P, T3], U32), tab2_words[0]),
-            load_words(placed("tab2_w1", [P, T3], U32, TAB2_W1_AT), tab2_words[1]),
-        ]
+        tab2_s = load_planes_packed("tab2_s", tab2_scales)
         load_w2(1, 1)
-        for g in range(SLICES, STEPS):
+        load_season(SLICES)
+        tab2_w = [load_words(held("tab2_w%d" % b, [P, T3], U32), tab2_words[b]) for b in range(HALVES)]
+        for g in range(SLICES + 1, STEPS):
             load_season(g)
         p1 = load_list("p1", pos1)
         p2 = load_list("p2", pos2)
@@ -128,30 +158,12 @@ def tile_list_mussel_host_scores_kernel(
             nc.sync.dma_start(out=scale_sb[:], in_=scale.rearrange("(m p) -> p m", p=P))
             nc.sync.dma_start(out=bias_sb[:], in_=bias.rearrange("(m p) -> p m", p=P))
         lim_sb = keep.tile([P, M_TILES, NP], F32, name="lim_sb", tag="w2_raw_0")
-        nc.sync.dma_start(out=lim_sb[:], in_=lim.rearrange("(m p) n -> p m n", p=P))
-
-        v_w = [held("v_w%d" % a, [P, S], U32) for a in range(PASSES)]
-        v_s = [held("v_s%d" % a, [P, S], U8) for a in range(PASSES)]
-
-        def gather_scales(a, first, last):
-            nc.vector.tensor_copy(v_s[a][:, first:last], tab_s[:, a, :].indirect(idx[:, first // 16 : last // 16]))
-
-        def gather_words(a, first, last):
-            nc.vector.tensor_copy(v_w[a][:, first:last], tab_w[a][:].indirect(idx[:, first // 16 : last // 16]))
-
-        w1_wp, w1_sp = {}, {}
-
-        def deal_w1_scales(b):
-            cols = slice(b * K_PASS, (b + 1) * K_PASS)
-            w1_sp[b] = held("w1_sp_%d" % b, [P, PASSES, PACK, P], U8)
-            nc.vector.tensor_copy(out=w1_sp[b][:], in_=w1_s[:, :, cols].rearrange("p a (m t) -> p a t m", t=PACK))
 
         def deal_w1_words(b):
-            cols = slice(b * K_PASS, (b + 1) * K_PASS)
             w1_wp[b] = held("w1_wp_%d" % b, [P, PASSES, PACK, P], U16)
             nc.scalar.copy(
                 out=w1_wp[b][:].rearrange("p a t m -> p a m t"),
-                in_=w1_w[:, :, cols].rearrange("p a (m t) -> p a m t", t=PACK),
+                in_=w1_w[:, :, b * K_PASS : (b + 1) * K_PASS].rearrange("p a (m t) -> p a m t", t=PACK),
             )
 
         w2_bf, w2_w, w2_s = {}, {}, {}
@@ -161,7 +173,8 @@ def tile_list_mussel_host_scores_kernel(
                 w2_bf[b, a] = placed("w2_bf_last", [P, PACK * K_PASS], BF16, W2_BF_AT)
             else:
                 w2_bf[b, a] = ring.tile([P, PACK * K_PASS], BF16, name="w2_bf", align_bytes=64)
-            nc.scalar.copy(
+            copy = nc.vector.tensor_copy if (b, a) == (0, 1) else nc.scalar.copy
+            copy(
                 out=w2_bf[b, a][:].rearrange("p (t m i) -> p m i t", t=PACK, i=PACK),
                 in_=w2_raw[b, a][:].rearrange("p i (m t) -> p m i t", t=PACK),
             )
@@ -172,7 +185,7 @@ def tile_list_mussel_host_scores_kernel(
             if b == 0:
                 w2_s[b, a] = held(name, [P, K_PASS], U8)
             else:
-                w2_s[b, a] = placed(name, [P, K_PASS], U8, TAB2_W1_AT if a == 1 else TAB2_S_AT)
+                w2_s[b, a] = placed(name, [P, K_PASS], U8, 2 * TURN * CHUNK_BYTES + a * K_PASS)
             nc.vector.quantize_mx(out=w2_w[b, a][:].bitcast(FP8X4), scales=w2_s[b, a][:], in_=w2_bf[b, a][:])
 
         two_sin2, low, h_bf, h_w, h_s = {}, {}, {}, {}, {}
@@ -191,13 +204,13 @@ def tile_list_mussel_host_scores_kernel(
                             out=z1[:, i, :],
                             lhsT=w1_wp[b][:, a, 2 * pair + i, :].bitcast(FP4X4),
                             lhsT_scale=w1_sp[b][:, a, 2 * pair + i, :],
-                            rhs=v_w[a][:, cols].bitcast(FP8X4),
-                            rhs_scale=v_s[a][:, cols],
+                            rhs=v_w[a, s].bitcast(FP8X4),
+                            rhs_scale=(v_s_low if a == 1 else v_s)[:, cols],
                             start=(a == 0),
                             stop=(a == PASSES - 1),
                         )
                 nc.vector.scalar_tensor_tensor(
-                    out=shifted[:, ts, :], in0=z1[:], scalar=math.pi / 2, in1=season_sb[g][:, ts, :],
+                    out=shifted[:, ts, :], in0=season_sb[g][:, ts, :], scalar=math.pi / 2, in1=z1[:],
                     op0=ALU.add, op1=ALU.add,
                 )
                 nc.scalar.activation(out=half_sin[:, ts, :], in_=shifted[:, ts, :], func=ACT.Sin, scale=0.5)
@@ -211,13 +224,9 @@ def tile_list_mussel_host_scores_kernel(
                     scale=math.sqrt(2.0),
                 )
 
-        def low_at(g):
-            slot = 2 if g % 2 == 0 and g > TURN else g % 2
-            return LOW_AT + slot * LOW_BYTES
-
         def lesser(g):
             b, s = divmod(g, SLICES)
-            low[g] = placed("low_%d" % g, [P, SLICE, PACK], F32, low_at(g))
+            low[g] = placed("low_%d" % g, [P, SLICE, PACK], F32, LOW_AT + g % 2 * LOW_BYTES)
             for u in range(SLICE // CHUNK):
                 cols = slice(s * SLICE + u * CHUNK, s * SLICE + (u + 1) * CHUNK)
                 z2 = psum.tile([P, PACK, CHUNK], F32, name="z2")
@@ -227,8 +236,8 @@ def tile_list_mussel_host_scores_kernel(
                             out=z2[:, t, :],
                             lhsT=w2_w[b, a][:, t * P : (t + 1) * P].bitcast(FP8X4),
                             lhsT_scale=w2_s[b, a][:, t * P : (t + 1) * P],
-                            rhs=v_w[a][:, cols].bitcast(FP8X4),
-                            rhs_scale=v_s[a][:, cols],
+                            rhs=v_w[a, s][:, u * CHUNK : (u + 1) * CHUNK].bitcast(FP8X4),
+                            rhs_scale=v_s[4 * a : P, cols],
                             start=(a == 0),
                             stop=(a == PASSES - 1),
                         )
@@ -237,17 +246,18 @@ def tile_list_mussel_host_scores_kernel(
                     in1=z2[:].rearrange("p t n -> p n t"), op0=ALU.add, op1=ALU.min,
                 )
 
-        def apply_gain(g):
-            b = g // SLICES
+        rounded = held("rounded", [P, SLICE + STRIP, PACK], BF16)
+        rounded_last = held("rounded_last", [P, SLICE, PACK], BF16)
+
+        def apply_gain(g, engine, first, last):
             if g == STEPS - 1:
-                h_bf[g] = held("h_bf_last", [P, SLICE, PACK], BF16)
+                h_bf[g] = rounded_last[:]
             else:
-                h_bf[g] = placed("h_bf_%d" % g, [P, SLICE, PACK], BF16, ROUNDED_AT)
-            engine = nc.vector if g == STEPS - 1 else nc.gpsimd
+                h_bf[g] = rounded[:, g % 2 * STRIP : g % 2 * STRIP + SLICE, :]
             engine.tensor_tensor(
-                out=h_bf[g][:],
-                in0=low[g][:],
-                in1=gain_sb[:, b : b + 1, :].to_broadcast([P, SLICE, PACK]),
+                out=h_bf[g][:, first:last, :],
+                in0=low[g][:, first:last, :],
+                in1=gain_sb[:, g // SLICES : g // SLICES + 1, :].to_broadcast([P, last - first, PACK]),
                 op=ALU.mult,
             )
 
@@ -261,28 +271,34 @@ def tile_list_mussel_host_scores_kernel(
             else:
                 h_s[g] = held("h_s_%d" % g, [P, SLICE], U8)
             nc.vector.quantize_mx(
-                out=h_w[g][:].bitcast(FP8X4), scales=h_s[g][:], in_=h_bf[g][:].rearrange("p n t -> p (n t)")
+                out=h_w[g][:].bitcast(FP8X4), scales=h_s[g][:], in_=h_bf[g].rearrange("p n t -> p (n t)")
             )
 
-        v2_w = {}
-        v2_s = {}
+        def after_step(g):
+            return (2 * g + 1) * CHUNK_BYTES + 4 * SLICE
 
-        def gather_strains():
-            v2_s[0] = placed("v2_s", [P, S2], U8, (2 * TURN + 1) * CHUNK_BYTES + 4 * SLICE)
-            nc.vector.tensor_copy(v2_s[0][:], tab2_s[:].indirect(idx2[:]))
-            for b in range(HALVES):
-                v2_w[b] = placed("v2_w%d" % b, [P, S2], U32, low_at(TURN - 1) + b * 4 * S2)
-                nc.vector.tensor_copy(v2_w[b][:], tab2_w[b][:].indirect(idx2[:]))
+        v2_w, v2_s = {}, {}
+        half = S2 // 2
+
+        def gather_strain_scales(part, at):
+            v2_s[part] = placed("v2_s%d" % part, [P, half], U8, at)
+            entries = idx2[:, part * half // 16 : (part + 1) * half // 16]
+            nc.vector.tensor_copy(v2_s[part][:], tab2_s[:].indirect(entries))
+
+        def gather_strain_words(b, part, at):
+            v2_w[b, part] = placed("v2_w%d_%d" % (b, part), [P, half], U32, at)
+            entries = idx2[:, part * half // 16 : (part + 1) * half // 16]
+            nc.vector.tensor_copy(v2_w[b, part][:], tab2_w[b][:].indirect(entries))
 
         e_sb = [held("e_%d" % m, [P, S], F32) for m in range(M_TILES)]
 
         def multiply_scores(m, s, sums):
-            rows = slice(m * P, (m + 1) * P)
+            part, rows = m // 2, slice(m % 2 * P, (m % 2 + 1) * P)
             for b in range(HALVES):
                 nc.tensor.matmul_mx(
                     out=sums,
-                    lhsT=v2_w[b][:, rows].bitcast(FP8X4),
-                    lhsT_scale=v2_s[0][4 * b : P, rows],
+                    lhsT=v2_w[b, part][:, rows].bitcast(FP8X4),
+                    lhsT_scale=v2_s[part][4 * b : P, rows],
                     rhs=h_w[b * SLICES + s][:].bitcast(FP8X4),
                     rhs_scale=h_s[b * SLICES + s][:],
                     start=(b == 0),
@@ -313,36 +329,47 @@ def tile_list_mussel_host_scores_kernel(
                 nc.sync.dma_start(out=out[m * P : (m + 1) * P, cols], in_=result[:])
 
         for b in range(HALVES):
-            deal_w1_scales(b)
-        gather_words(0, 0, S)
-        gather_words(1, 0, S)
-        for a in range(PASSES):
-            gather_scales(a, 0, SLICE)
-        for b in range(HALVES):
             deal_w1_words(b)
-        for a in range(PASSES):
-            round_w2(0, a)
+        round_w2(0, 0)
         quantise_w2(0, 0)
         wave(0)
-        gather_scales(0, SLICE, S)
+        round_w2(0, 1)
         quantise_w2(0, 1)
-        gather_scales(1, SLICE, S)
         for g in range(STEPS):
             if 0 <= g - (TURN - 1) < PASSES:
                 round_w2(1, g - (TURN - 1))
             if g + 1 < STEPS:
                 wave(g + 1)
             lesser(g)
+            if g == 1:
+                gather_words(1, placed("v_w1_last", [P, SLICE], U32, after_step(g)), S - SLICE, S)
+            if g in (2, 3):
+                gather_strain_scales(g - 2, after_step(g))
             if g == TURN:
-                gather_strains()
                 for a in range(PASSES):
                     quantise_w2(1, a)
-            if g > 0:
+                nc.sync.dma_start(out=lim_sb[:], in_=lim.rearrange("(m p) n -> p m n", p=P))
+            if g == 4:
+                gather_strain_words(0, 0, 2 * g * CHUNK_BYTES)
+                gather_strain_words(1, 0, after_step(g))
+            if g in (5, 6):
+                gather_strain_words(g - 5, 1, after_step(g))
+            if g + 1 < STEPS:
+                strip = (0, STRIP) if g % 2 == 0 else (SLICE - STRIP, SLICE)
+                rest = (STRIP, SLICE) if g % 2 == 0 else (0, SLICE - STRIP)
+                apply_gain(g, nc.vector, *strip)
+                if g > 0:
+                    quantise_h(g - 1)
+                apply_gain(g, nc.gpsimd, *rest)
+            else:
                 quantise_h(g - 1)
-            apply_gain(g)
-            if SLICES < g < STEPS - 1:
-                for first in range(0, M_TILES, 2):
-                    scores(g - 1 - SLICES, [first, first + 1])
+                apply_gain(g, nc.vector, 0, SLICE)
+            if g == 5:
+                scores(0, [0, 1])
+            if g == 6:
+                scores(0, [2, 3])
+                scores(1, [0, 1])
+                scores(1, [2, 3])
         scores(SLICES - 2, [0])
         last_two = [psum.tile([P, 2, SLICE], F32, name="z1") for m in range(1, M_TILES)]
         for m in range(1, M_TILES):
@@ -355,5 +382,6 @@ def tile_list_mussel_host_scores_kernel(
             multiply_scores(m, SLICES - 1, last_two[m - 1][:, 1, :])
         finish(0, 2)
         for m in range(1, M_TILES):
-            nc.scalar.copy(out=e_sb[m][:, S - 2 * SLICE :], in_=last_two[m - 1][:].rearrange("p s j -> p (s j)"))
+            copy = nc.vector.tensor_copy if m == 1 else nc.scalar.copy
+            copy(out=e_sb[m][:, S - 2 * SLICE :], in_=last_two[m - 1][:].rearrange("p s j -> p (s j)"))
             finish(m, 2 if m == M_TILES - 1 else 1)

import math
from contextlib import ExitStack

import concourse.mybir as mybir

K, H, T, S, T3, S2, NP = 1024, 1024, 2048, 1024, 2048, 512, 512
FLOPS = 2 * (2 * K * H * S + H * S2 * S)

F32 = mybir.dt.float32
BF16 = mybir.dt.bfloat16
I32 = mybir.dt.int32
U32 = mybir.dt.uint32
U16 = mybir.dt.uint16
U8 = mybir.dt.uint8
FP8X4 = mybir.dt.float8_e4m3fn_x4
FP4X4 = mybir.dt.float4_e2m1fn_x4
ACT = mybir.ActivationFunctionType
ALU = mybir.AluOpType

P = 128
PACK = 4
K_PASS = P * PACK
PASSES = K // K_PASS
HALVES = H // K_PASS
CHUNK = 128
SLICE = 256
SLICES = S // SLICE
STEPS = HALVES * SLICES
M_TILES = S2 // P
QUADS = 4

CHUNK_BYTES = CHUNK * PACK * 4
LOW_AT = 2 * STEPS * CHUNK_BYTES
LOW_BYTES = SLICE * PACK * 4
W2_BF_AT = LOW_AT + 2 * LOW_BYTES
STRIP = 64
TURN = SLICES - 1
MOVED_ROWS = 112


def tile_list_mussel_host_scores_kernel(
    tc, tab_words, tab_scales, tab2_words, tab2_scales, w1_words, w1_scales, w2, season, gain, scale, bias, lim,
    offs, offs2, pos1, pos2, out,
):
    nc = tc.nc
    with ExitStack() as ctx:
        lists = ctx.enter_context(tc.tile_pool(name="lists", bufs=1))
        keep = ctx.enter_context(tc.tile_pool(name="keep", bufs=1))
        ring = ctx.enter_context(tc.tile_pool(name="ring", bufs=2))
        reuse = ctx.enter_context(tc.tile_pool(name="reuse", bufs=1))
        psum = ctx.enter_context(tc.psum_pool(name="psum", bufs=3))
        psum_e = ctx.enter_context(tc.psum_pool(name="psum_e", bufs=2))

        def held(name, shape, dtype):
            return keep.tile(shape, dtype, name=name, align_bytes=64)

        def placed(name, shape, dtype, offset):
            return reuse.tile(shape, dtype, name=name, align_bytes=64, offset=offset)

        def load_list(name, src):
            tile = lists.tile(list(src.shape), U16, name=name)
            nc.sync.dma_start(tile[:], src)
            return tile

        def load_words(tile, src):
            nc.sync.dma_start(out=tile[:].bitcast(I32), in_=src.rearrange("p t i -> p (t i)").bitcast(I32))
            return tile

        def load_planes_side_by_side(name, src, clear):
            tile = held(name, [P, PASSES, src.shape[2]], U8)
            clear.memset(tile[:].rearrange("p a t -> p (a t)").bitcast(I32), 0)
            for q in range(QUADS):
                nc.sync.dma_start(
                    out=tile[32 * q : 32 * q + 4, :, :].bitcast(I32),
                    in_=src[:, 4 * q : 4 * q + 4, :].rearrange("a r t -> r a t").bitcast(I32),
                )
            return tile

        def load_planes_packed(name, src):
            tile = held(name, [P, src.shape[2]], U8)
            nc.vector.memset(tile[:].bitcast(I32), 0)
            for q in range(QUADS):
                nc.sync.dma_start(
                    out=tile[32 * q : 32 * q + 8, :].bitcast(I32), in_=src[:, 4 * q : 4 * q + 4, :].bitcast(I32)
                )
            return tile

        w2_raw, season_sb = {}, {}

        def load_w2(b, a):
            w2_raw[b, a] = keep.tile([P, PACK, K_PASS], F32, name="w2_raw_%d_%d" % (b, a), tag="w2_raw_%d" % a)
            rows = w2[a * K_PASS : (a + 1) * K_PASS, b * K_PASS : (b + 1) * K_PASS]
            nc.sync.dma_start(out=w2_raw[b, a][:], in_=rows.rearrange("(p i) c -> p i c", i=PACK))

        def load_season(g):
            b, s = divmod(g, SLICES)
            season_sb[g] = held("season_%d" % g, [P, PACK, SLICE], F32)
            rows = season[b * K_PASS : (b + 1) * K_PASS, s * SLICE : (s + 1) * SLICE]
            nc.sync.dma_start(out=season_sb[g][:], in_=rows.rearrange("(p t) j -> p t j", t=PACK))

        idx = load_list("idx", offs)
        w1_s = load_planes_side_by_side("w1_s", w1_scales, nc.vector)
        tab_w = [load_words(held("tab_w%d" % a, [P, T], U32), tab_words[a]) for a in range(PASSES)]
        w1_w = held("w1_w", [P, PASSES, H], U16)
        nc.sync.dma_start(out=w1_w[:].bitcast(I32), in_=w1_words.rearrange("a p c -> p a c").bitcast(I32))
        tab_s = load_planes_packed("tab_s", tab_scales)
        load_w2(0, 0)
        load_season(0)

        w1_wp, w1_sp = {}, {}

        def deal_w1_scales(b):
            cols = slice(b * K_PASS, (b + 1) * K_PASS)
            w1_sp[b] = held("w1_sp_%d" % b, [P, PASSES, PACK, P], U8)
            nc.vector.tensor_copy(out=w1_sp[b][:], in_=w1_s[:, :, cols].rearrange("p a (m t) -> p a t m", t=PACK))

        v_w = {}
        v_s = held("v_s", [P, S], U8)
        v_s_low = held("v_s_low", [P, S], U8)
        nc.vector.memset(v_s_low[96:P, :].bitcast(I32), 0)

        def gather_scales(first, last):
            nc.vector.tensor_copy(v_s[:, first:last], tab_s[:].indirect(idx[:, first // 16 : last // 16]))
            nc.sync.dma_start(
                out=v_s_low[0:MOVED_ROWS, first:last].bitcast(I32), in_=v_s[4 : 4 + MOVED_ROWS, first:last].bitcast(I32)
            )

        def gather_words(a, tile, first, last):
            nc.vector.tensor_copy(tile[:], tab_w[a][:].indirect(idx[:, first // 16 : last // 16]))
            for s in range(first // SLICE, last // SLICE):
                v_w[a, s] = tile[:, s * SLICE - first : (s + 1) * SLICE - first]

        for b in range(HALVES):
            deal_w1_scales(b)
        gather_words(0, held("v_w0", [P, S], U32), 0, S)
        gather_words(1, held("v_w1", [P, S - SLICE], U32), 0, S - SLICE)
        gather_scales(0, SLICE)
        load_w2(0, 1)
        gather_scales(SLICE, S)
        load_season(1)
        gain_sb = held("gain_sb", [P, HALVES, PACK], F32)
        nc.sync.dma_start(out=gain_sb[:], in_=gain.rearrange("(b p t) -> p b t", b=HALVES, t=PACK))
        for g in range(2, SLICES):
            load_season(g)
        load_w2(1, 0)
        idx2 = load_list("idx2", offs2)
        tab2_s = load_planes_packed("tab2_s", tab2_scales)
        load_w2(1, 1)
        load_season(SLICES)
        tab2_w = [load_words(held("tab2_w%d" % b, [P, T3], U32), tab2_words[b]) for b in range(HALVES)]
        for g in range(SLICES + 1, STEPS):
            load_season(g)
        p1 = load_list("p1", pos1)
        p2 = load_list("p2", pos2)
        scale_sb = held("scale_sb", [P, M_TILES], F32)
        bias_sb = held("bias_sb", [P, M_TILES], F32)
        with nc.allow_non_contiguous_dma(reason="one value a strain, strains on the partitions"):
            nc.sync.dma_start(out=scale_sb[:], in_=scale.rearrange("(m p) -> p m", p=P))
            nc.sync.dma_start(out=bias_sb[:], in_=bias.rearrange("(m p) -> p m", p=P))
        lim_sb = keep.tile([P, M_TILES, NP], F32, name="lim_sb", tag="w2_raw_0")

        def deal_w1_words(b):
            w1_wp[b] = held("w1_wp_%d" % b, [P, PASSES, PACK, P], U16)
            nc.scalar.copy(
                out=w1_wp[b][:].rearrange("p a t m -> p a m t"),
                in_=w1_w[:, :, b * K_PASS : (b + 1) * K_PASS].rearrange("p a (m t) -> p a m t", t=PACK),
            )

        w2_bf, w2_w, w2_s = {}, {}, {}

        def round_w2(b, a):
            if (b, a) == (1, 1):
                w2_bf[b, a] = placed("w2_bf_last", [P, PACK * K_PASS], BF16, W2_BF_AT)
            else:
                w2_bf[b, a] = ring.tile([P, PACK * K_PASS], BF16, name="w2_bf", align_bytes=64)
            copy = nc.vector.tensor_copy if (b, a) == (0, 1) else nc.scalar.copy
            copy(
                out=w2_bf[b, a][:].rearrange("p (t m i) -> p m i t", t=PACK, i=PACK),
                in_=w2_raw[b, a][:].rearrange("p i (m t) -> p m i t", t=PACK),
            )

        def quantise_w2(b, a):
            w2_w[b, a] = held("w2_w_%d_%d" % (b, a), [P, K_PASS], U32)
            name = "w2_s_%d_%d" % (b, a)
            if b == 0:
                w2_s[b, a] = held(name, [P, K_PASS], U8)
            else:
                w2_s[b, a] = placed(name, [P, K_PASS], U8, 2 * TURN * CHUNK_BYTES + a * K_PASS)
            nc.vector.quantize_mx(out=w2_w[b, a][:].bitcast(FP8X4), scales=w2_s[b, a][:], in_=w2_bf[b, a][:])

        two_sin2, low, h_bf, h_w, h_s = {}, {}, {}, {}, {}

        def wave(g):
            b, s = divmod(g, SLICES)
            cols = slice(s * SLICE, (s + 1) * SLICE)
            shifted = ring.tile([P, PACK, SLICE], F32, name="shifted")
            half_sin = ring.tile([P, PACK, SLICE], F32, name="half_sin")
            for pair in range(PACK // 2):
                ts = slice(2 * pair, 2 * pair + 2)
                z1 = psum.tile([P, 2, SLICE], F32, name="z1")
                for i in range(2):
                    for a in range(PASSES):
                        nc.tensor.matmul_mx(
                            out=z1[:, i, :],
                            lhsT=w1_wp[b][:, a, 2 * pair + i, :].bitcast(FP4X4),
                            lhsT_scale=w1_sp[b][:, a, 2 * pair + i, :],
                            rhs=v_w[a, s].bitcast(FP8X4),
                            rhs_scale=(v_s_low if a == 1 else v_s)[:, cols],
                            start=(a == 0),
                            stop=(a == PASSES - 1),
                        )
                nc.vector.scalar_tensor_tensor(
                    out=shifted[:, ts, :], in0=season_sb[g][:, ts, :], scalar=math.pi / 2, in1=z1[:],
                    op0=ALU.add, op1=ALU.add,
                )
                nc.scalar.activation(out=half_sin[:, ts, :], in_=shifted[:, ts, :], func=ACT.Sin, scale=0.5)
            for u in range(SLICE // CHUNK):
                c = 2 * g + u
                two_sin2[c] = placed("two_sin2_%d" % c, [P, CHUNK, PACK], F32, c * CHUNK_BYTES)
                nc.scalar.activation(
                    out=two_sin2[c][:].rearrange("p (n i) t -> p n t i", i=4),
                    in_=half_sin[:, :, u * CHUNK : (u + 1) * CHUNK].rearrange("p t (n i) -> p n t i", i=4),
                    func=ACT.Square,
                    scale=math.sqrt(2.0),
                )

        def lesser(g):
            b, s = divmod(g, SLICES)
            low[g] = placed("low_%d" % g, [P, SLICE, PACK], F32, LOW_AT + g % 2 * LOW_BYTES)
            for u in range(SLICE // CHUNK):
                cols = slice(s * SLICE + u * CHUNK, s * SLICE + (u + 1) * CHUNK)
                z2 = psum.tile([P, PACK, CHUNK], F32, name="z2")
                for t in range(PACK):
                    for a in range(PASSES):
                        nc.tensor.matmul_mx(
                            out=z2[:, t, :],
                            lhsT=w2_w[b, a][:, t * P : (t + 1) * P].bitcast(FP8X4),
                            lhsT_scale=w2_s[b, a][:, t * P : (t + 1) * P],
                            rhs=v_w[a, s][:, u * CHUNK : (u + 1) * CHUNK].bitcast(FP8X4),
                            rhs_scale=v_s[4 * a : P, cols],
                            start=(a == 0),
                            stop=(a == PASSES - 1),
                        )
                nc.vector.scalar_tensor_tensor(
                    out=low[g][:, u * CHUNK : (u + 1) * CHUNK, :], in0=two_sin2[2 * g + u][:], scalar=-1.0,
                    in1=z2[:].rearrange("p t n -> p n t"), op0=ALU.add, op1=ALU.min,
                )

        rounded = held("rounded", [P, SLICE + STRIP, PACK], BF16)
        rounded_last = held("rounded_last", [P, SLICE, PACK], BF16)

        def apply_gain(g, engine, first, last):
            if g == STEPS - 1:
                h_bf[g] = rounded_last[:]
            else:
                h_bf[g] = rounded[:, g % 2 * STRIP : g % 2 * STRIP + SLICE, :]
            engine.tensor_tensor(
                out=h_bf[g][:, first:last, :],
                in0=low[g][:, first:last, :],
                in1=gain_sb[:, g // SLICES : g // SLICES + 1, :].to_broadcast([P, last - first, PACK]),
                op=ALU.mult,
            )

        def quantise_h(g):
            if g + 1 < STEPS:
                h_w[g] = placed("h_w_%d" % g, [P, SLICE], U32, (2 * g + 3) * CHUNK_BYTES)
            else:
                h_w[g] = held("h_w_last", [P, SLICE], U32)
            if g == TURN - 1:
                h_s[g] = placed("h_s_%d" % g, [P, SLICE], U8, W2_BF_AT)
            else:
                h_s[g] = held("h_s_%d" % g, [P, SLICE], U8)
            nc.vector.quantize_mx(
                out=h_w[g][:].bitcast(FP8X4), scales=h_s[g][:], in_=h_bf[g].rearrange("p n t -> p (n t)")
            )

        def after_step(g):
            return (2 * g + 1) * CHUNK_BYTES + 4 * SLICE

        v2_w, v2_s = {}, {}
        half = S2 // 2

        def gather_strain_scales(part, at):
            v2_s[part] = placed("v2_s%d" % part, [P, half], U8, at)
            entries = idx2[:, part * half // 16 : (part + 1) * half // 16]
            nc.vector.tensor_copy(v2_s[part][:], tab2_s[:].indirect(entries))

        def gather_strain_words(b, part, at):
            v2_w[b, part] = placed("v2_w%d_%d" % (b, part), [P, half], U32, at)
            entries = idx2[:, part * half // 16 : (part + 1) * half // 16]
            nc.vector.tensor_copy(v2_w[b, part][:], tab2_w[b][:].indirect(entries))

        e_sb = [held("e_%d" % m, [P, S], F32) for m in range(M_TILES)]

        def multiply_scores(m, s, sums):
            part, rows = m // 2, slice(m % 2 * P, (m % 2 + 1) * P)
            for b in range(HALVES):
                nc.tensor.matmul_mx(
                    out=sums,
                    lhsT=v2_w[b, part][:, rows].bitcast(FP8X4),
                    lhsT_scale=v2_s[part][4 * b : P, rows],
                    rhs=h_w[b * SLICES + s][:].bitcast(FP8X4),
                    rhs_scale=h_s[b * SLICES + s][:],
                    start=(b == 0),
                    stop=(b == HALVES - 1),
                )

        def scores(s, tiles):
            bank = psum_e.tile([P, len(tiles), SLICE], F32, name="e_bank")
            for i, m in enumerate(tiles):
                multiply_scores(m, s, bank[:, i, :])
            for i, m in enumerate(tiles):
                nc.scalar.copy(out=e_sb[m][:, s * SLICE : (s + 1) * SLICE], in_=bank[:, i, :])

        def finish(m, parts):
            width = NP // parts
            for part in range(parts):
                entries = slice(part * width // 16, (part + 1) * width // 16)
                cols = slice(part * width, (part + 1) * width)
                look = ring.tile([P, width], F32, name="look", bufs=3)
                nc.scalar.activation(
                    out=look[:], in_=e_sb[m][:].indirect(p1[:, entries]), func=ACT.Exp,
                    bias=bias_sb[:, m : m + 1], scale=scale_sb[:, m : m + 1],
                )
                product = ring.tile([P, width], F32, name="product")
                nc.vector.tensor_tensor(product[:], e_sb[m][:].indirect(p2[:, entries]), look[:], ALU.mult)
                result = ring.tile([P, width], F32, name="result", bufs=4)
                nc.vector.tensor_tensor(result[:], product[:], lim_sb[:, m, cols], ALU.min)
                nc.sync.dma_start(out=out[m * P : (m + 1) * P, cols], in_=result[:])

        for b in range(HALVES):
            deal_w1_words(b)
        round_w2(0, 0)
        quantise_w2(0, 0)
        wave(0)
        round_w2(0, 1)
        quantise_w2(0, 1)
        for g in range(STEPS):
            if 0 <= g - (TURN - 1) < PASSES:
                round_w2(1, g - (TURN - 1))
            if g + 1 < STEPS:
                wave(g + 1)
            lesser(g)
            if g == 1:
                gather_words(1, placed("v_w1_last", [P, SLICE], U32, after_step(g)), S - SLICE, S)
            if g in (2, 3):
                gather_strain_scales(g - 2, after_step(g))
            if g == TURN:
                for a in range(PASSES):
                    quantise_w2(1, a)
                nc.sync.dma_start(out=lim_sb[:], in_=lim.rearrange("(m p) n -> p m n", p=P))
            if g == 4:
                gather_strain_words(0, 0, 2 * g * CHUNK_BYTES)
                gather_strain_words(1, 0, after_step(g))
            if g in (5, 6):
                gather_strain_words(g - 5, 1, after_step(g))
            if g + 1 < STEPS:
                strip = (0, STRIP) if g % 2 == 0 else (SLICE - STRIP, SLICE)
                rest = (STRIP, SLICE) if g % 2 == 0 else (0, SLICE - STRIP)
                apply_gain(g, nc.vector, *strip)
                if g > 0:
                    quantise_h(g - 1)
                apply_gain(g, nc.gpsimd, *rest)
            else:
                quantise_h(g - 1)
                apply_gain(g, nc.vector, 0, SLICE)
            if g == 5:
                scores(0, [0, 1])
            if g == 6:
                scores(0, [2, 3])
                scores(1, [0, 1])
                scores(1, [2, 3])
        scores(SLICES - 2, [0])
        last_two = [psum.tile([P, 2, SLICE], F32, name="z1") for m in range(1, M_TILES)]
        for m in range(1, M_TILES):
            multiply_scores(m, SLICES - 2, last_two[m - 1][:, 0, :])
        quantise_h(STEPS - 1)
        first_bank = psum_e.tile([P, SLICE], F32, name="e_bank")
        multiply_scores(0, SLICES - 1, first_bank[:])
        nc.vector.tensor_copy(out=e_sb[0][:, S - SLICE :], in_=first_bank[:])
        for m in range(1, M_TILES):
            multiply_scores(m, SLICES - 1, last_two[m - 1][:, 1, :])
        finish(0, 2)
        for m in range(1, M_TILES):
            copy = nc.vector.tensor_copy if m == 1 else nc.scalar.copy
            copy(out=e_sb[m][:, S - 2 * SLICE :], in_=last_two[m - 1][:].rearrange("p s j -> p (s j)"))
            finish(m, 2 if m == M_TILES - 1 else 1)
